import numpy as np
import ml_dtypes


def mxq(x, axis, fmt="e4m3"):
    dtype, down = {"e4m3": (ml_dtypes.float8_e4m3fn, 7), "e5m2": (ml_dtypes.float8_e5m2, 14)}[fmt]
    v = np.moveaxis(np.asarray(x, np.float32).astype(ml_dtypes.bfloat16).astype(np.float64), axis, -1)
    blocks = v.reshape(v.shape[:-1] + (-1, 32))
    amax = np.abs(blocks).max(-1, keepdims=True)
    byte = np.maximum(np.where(amax > 0, np.frexp(amax)[1] - 1 + 127, 0) - down, 1)
    scale = np.exp2(byte - 127.0)
    codes = (blocks / scale).astype(np.float32).astype(dtype).astype(np.float64)
    return np.moveaxis((codes * scale).reshape(v.shape), -1, axis)


WIDE = False


def mx_kscale(k):
    if not WIDE:
        return np.ones(k)
    levels = np.array([10, -10, 5, -5, 0])
    if k % 512:
        return np.exp2(np.random.permutation(np.resize(levels, k // 32))).repeat(32)
    a = np.empty((k // 512, 16))
    for p in range(k // 512):
        a[p, :8] = np.random.permutation(np.resize(levels, 8))
        for g in range(8):
            far = levels[np.abs(levels - a[p, g]) >= 10]
            a[p, g + 8] = far[np.random.randint(len(far))]
    return np.exp2(a.ravel()).repeat(32)


BF16 = ml_dtypes.bfloat16


def bf(x):
    return np.asarray(x, np.float32).astype(BF16)


def f64(x):
    return np.asarray(x).astype(np.float64)


E2M1 = np.array([0.0, 0.5, 1.0, 1.5, 2.0, 3.0, 4.0, 6.0, -0.0, -0.5, -1.0, -1.5, -2.0, -3.0, -4.0, -6.0])


def pack_weight(w, fmt):
    k, n = w.shape
    w = f64(bf(w)).reshape(k // 32, 32, n)
    amax = np.abs(w).max(1)
    if fmt == "e4m3":
        byte = np.frexp(amax)[1] - 1 + 127 - 7
    else:
        mant, ex = np.frexp(amax / 6.0)
        byte = np.where(mant > 0.5, ex, ex - 1) + 127
    byte = np.clip(np.where(amax > 0, byte, 1), 1, 254)
    scaled = (w * np.exp2(127.0 - byte)[:, None, :]).reshape(k, n).astype(np.float32)
    by_word = np.ascontiguousarray(scaled.reshape(k // 512, 128, 4, n).transpose(0, 1, 3, 2))
    if fmt == "e4m3":
        words = by_word.astype(ml_dtypes.float8_e4m3fn).view(np.uint8)
    else:
        c = by_word.astype(ml_dtypes.float4_e2m1fn).view(np.uint8) & 0xF
        words = c[..., 0::2] | (c[..., 1::2] << 4)
    return np.ascontiguousarray(words), np.ascontiguousarray(byte.astype(np.uint8).reshape(k // 512, 16, n))


def unpack_weight(words, scales, fmt):
    g, p, n, _ = words.shape
    if fmt == "e4m3":
        vals = np.ascontiguousarray(words).view(ml_dtypes.float8_e4m3fn).astype(np.float64)
    else:
        nib = np.empty((g, p, n, 4), np.uint8)
        nib[..., 0::2] = words & 0xF
        nib[..., 1::2] = words >> 4
        vals = E2M1[nib]
    vals = vals * np.repeat(np.exp2(scales.astype(np.float64) - 127.0), 8, axis=1)[..., None]
    return vals.transpose(0, 1, 3, 2).reshape(g * 512, n)
def pack4(w):
    words, scales = pack_weight(w, "e2m1")
    return words.reshape(words.shape[0], 128, -1), scales


def unpack4(words, scales):
    return unpack_weight(words.reshape(words.shape[0], 128, -1, 2), scales, "e2m1")


def planes(Y):
    n, m = Y.shape
    b = f64(bf(Y)).reshape(n // 32, 32, m)
    amax = np.abs(b).max(1)
    byte = np.clip(np.where(amax > 0, np.frexp(amax)[1] - 1 + 127 - 7, 1), 1, 254)
    codes = (b * np.exp2(127.0 - byte)[:, None, :]).reshape(n, m).astype(np.float32).astype(ml_dtypes.float8_e4m3fn).view(np.uint8)
    words = codes.reshape(n // 512, 128, 4, m).transpose(0, 1, 3, 2)
    return np.ascontiguousarray(words), np.ascontiguousarray(byte.astype(np.uint8).reshape(n // 512, 16, m))


E, C, D, F = 4, 384, 1024, 1536

def setup_inputs():
    s = mx_kscale(D)
    t = mx_kscale(F)
    spread = np.exp(0.8 * np.random.randn(D))
    x = np.random.randn(D, E * C) * s[:, None]
    up = np.random.randn(D, E * F) / np.sqrt(D) / s[:, None] * np.tile(t, E)[None, :]
    down = np.random.randn(E, F, D) * np.sqrt(2.0 / F) * spread / t[None, :, None]
    x_words, x_scales = pack_weight(x, "e4m3")
    up_words, up_scales = pack4(up)
    return {
        "x_words": x_words,
        "x_scales": x_scales,
        "up_words": up_words,
        "up_scales": up_scales,
        "b_up": bf(0.3 * np.random.randn(E, F) * t[None, :]),
        "down": bf(down),
        "b_down": bf(0.3 * np.random.randn(E, D) * spread),
        "gate_logit": bf(0.5 + np.random.randn(E, C)),
        "skip": bf(0.5 * np.random.randn(E, C, D) * spread),
    }

def reference(x_words, x_scales, up_words, up_scales, b_up, down, b_down, gate_logit, skip):
    x = unpack_weight(x_words, x_scales, "e4m3").reshape(D, E, C).transpose(1, 2, 0)
    up = unpack4(up_words, up_scales).reshape(D, E, F).transpose(1, 0, 2)
    h = np.maximum((x @ up) + f64(b_up)[:, None, :], 0.0)
    o = mxq(h, 2, "e4m3") @ mxq(f64(down), 1, "e4m3")
    gate = 1.0 / (1.0 + np.exp(-f64(gate_logit)))
    y = f64(skip) + gate[:, :, None] * (o + f64(b_down)[:, None, :])
    Y = y.reshape(E * C, D).T
    words, scales = planes(Y)
    return y, words, scales

from contextlib import ExitStack

import concourse.mybir as mybir
from concourse.masks import make_identity

E, C, D, F = 4, 384, 1024, 1536
FLOPS = 2 * 2 * E * C * D * F

F32 = mybir.dt.float32
BF16 = mybir.dt.bfloat16
I32 = mybir.dt.int32
U32 = mybir.dt.uint32
U8 = mybir.dt.uint8
FP8X4 = mybir.dt.float8_e4m3fn_x4
FP4X4 = mybir.dt.float4_e2m1fn_x4
ACT = mybir.ActivationFunctionType
ALU = mybir.AluOpType

P = 128
KP = 512
GROUPS = F // KP
STEPS = E * GROUPS
TILES = C // P
GATE_ROW = 32
V_COLS = [704,736,320,544,864,768,320,768,832,896,480,480]
MODE = "D"
CAST_V = [4,5,6,8,11]
BUFS = {"d_raw":5,"d_mix":3,"dc":7,"h_bank":2,"o_bank":2,"b_bank":2,"t_bank":2,"base":10,"y_sb":3,"hc":5,"ot":2,"skip":3}
BDOWN_ROW = 64
D_TILES = [[0, 1, 2], [3, 4, 5], [6, 7]]
ORDER = [
    ("back0", 3),
    ("store_planes", 8),
    ("oo1", 1),
    ("h_mix", -2),
    ("d_s1", -1),
    ("h_out1", -3),
    ("load_down", -3),
    ("y1", 4),
    ("load_skip", 3),
    ("turn_out", 6),
    ("dq0", -2),
    ("h_q", -2),
    ("back1", 3),
    ("oo2", 1),
    ("d_v", -3),
    ("load_x", -4),
    ("store_y", 5),
    ("load_consts", -5),
    ("load_xs", -4),
    ("turn", 5),
    ("d_s0", -3),
    ("y_q", 7),
    ("cast", 4),
    ("m20", 0),
    ("load_up", -5),
    ("consts", -4),
    ("dq1", -1),
    ("m1a", -4),
    ("load_us", -5),
    ("m21", 0),
    ("m1b", -4),
    ("h_out0", -4),
    ("m22", 0),
    ("oo0", 0),
    ("perm", -5),
    ("y0", 3),
]


def tile_routed_relu_experts_h2_kernel(tc, x_words, x_scales, up_words, up_scales, b_up, down, b_down,
                                                  gate_logit, skip, out_0, out_1, out_2):
    nc = tc.nc
    with ExitStack() as ctx:
        keep = ctx.enter_context(tc.tile_pool(name="keep", bufs=1))
        work = ctx.enter_context(tc.tile_pool(name="work", bufs=2))
        psum = ctx.enter_context(tc.psum_pool(name="psum", bufs=1))
        ctx.enter_context(tc.manual_schedule())

        xw_hbm = x_words.rearrange("k p n t -> p k (n t)")
        upw_hbm = up_words.rearrange("k p n -> p k n")
        yw_hbm = out_1.rearrange("g p m t -> p g (m t)")

        def move_scale_rows(queue, plane, rows, cols, to_hbm):
            for q in range(4):
                sb = plane[32 * q : 32 * q + 4, :, :].bitcast(I32)
                hbm = rows[:, 4 * q : 4 * q + 4, cols].rearrange("k r n -> r k n").bitcast(I32)
                if to_hbm:
                    queue.dma_start(out=hbm, in_=sb)
                else:
                    queue.dma_start(out=sb, in_=hbm)

        t = {}

        xs_first = keep.tile([P, 2, C], U8, name="xs_first", align_bytes=64)
        xs_rest = keep.tile([P, 2, (E - 1) * C], U8, name="xs_rest", align_bytes=64)
        us_raw = [keep.tile([P, 2, F], U8, name="us_raw%d" % i, align_bytes=64) for i in range(2)]
        ys_head = keep.tile([P, 2, (E - 1) * C], U8, name="ys_head", align_bytes=64)
        ys_last = keep.tile([P, 2, C], U8, name="ys_last", align_bytes=64)
        rows = keep.tile([P, KP], BF16, name="rows")
        rows32 = keep.tile([P, 4, P], F32, name="rows32")
        ident = keep.tile([P, P], F32, name="ident")
        consts = keep.tile([P, 4, BDOWN_ROW + 32], F32, name="consts")

        def load_down(s):
            e, g = divmod(s, GROUPS)
            raw = work.tile([P, 4, D], BF16, name="d_raw", bufs=BUFS["d_raw"])
            src = down[e, KP * g : KP * (g + 1), :].rearrange("(m t r) d -> r m t d", t=4, r=4)
            for r in range(4):
                nc.sync.dma_start(out=raw[r:P:4, :, :], in_=src[r])
            t["d_raw", s] = raw

        def load_up(s):
            raw = work.tile([P, 2, 2 * KP], U8, name="upw_raw", bufs=3, align_bytes=64)
            nc.sync.dma_start(out=raw[:].bitcast(I32), in_=upw_hbm[:, :, 2 * KP * s : 2 * KP * (s + 1)].bitcast(I32))
            t["upw_raw", s] = raw

        def load_x(s):
            e, g = divmod(s, GROUPS)
            if g == 0:
                xw = work.tile([P, 2, C], U32, name="xw", bufs=2, align_bytes=64)
                nc.sync.dma_start(out=xw[:].bitcast(I32), in_=xw_hbm[:, :, 4 * C * e : 4 * C * (e + 1)].bitcast(I32))
                t["xw", e] = xw

        def load_us(s):
            e, g = divmod(s, GROUPS)
            if g == 0:
                assert e < 2 or ("upw", GROUPS * (e - 2) + 2) in t
                move_scale_rows(nc.sync, us_raw[e % 2], up_scales, slice(F * e, F * (e + 1)), False)
                t["us", e] = us_raw[e % 2]

        def load_xs(s):
            if s == 0:
                move_scale_rows(nc.sync, xs_first, x_scales, slice(0, C), False)
                t["xs", 0] = xs_first
            if s == GROUPS:
                move_scale_rows(nc.sync, xs_rest, x_scales, slice(C, E * C), False)
                for e in range(1, E):
                    t["xs", e] = xs_rest

        def load_skip(s):
            e, j = divmod(s, TILES)
            if j == 0:
                if MODE == "T":
                    bias = work.tile([P, D], BF16, name="b_bc", bufs=2)
                    nc.sync.dma_start(out=bias[:], in_=b_down[e].partition_broadcast(P))
                    t["b_bc", e] = bias
                sk = work.tile([P, TILES, D], BF16, name="skip_sb", bufs=BUFS["skip"])
                nc.sync.dma_start(out=sk[:], in_=skip[e].rearrange("(j p) d -> p j d", p=P))
                t["skip", e] = sk

        def load_consts(s):
            if s == 0:
                nc.scalar.dma_start(out=rows[GATE_ROW : GATE_ROW + STEPS, 0:P], in_=gate_logit.rearrange("e (j c) -> (e j) c", c=P))
                nc.scalar.dma_start(out=rows[0:STEPS, :], in_=b_up.rearrange("e (g f) -> (e g) f", f=KP))
                if MODE == "D":
                    nc.scalar.dma_start(out=rows[BDOWN_ROW : BDOWN_ROW + 32, 0:P], in_=b_down.rearrange("e (i d) -> (e i) d", d=P))
                t["rows"] = rows

        def make_consts(s):
            if s == 0:
                src = t["rows"]
                nc.scalar.activation(out=rows32[GATE_ROW : GATE_ROW + STEPS, 0, :], in_=src[GATE_ROW : GATE_ROW + STEPS, 0:P], func=ACT.Sigmoid)
                nc.vector.tensor_copy(out=rows32[0:STEPS, :, :].rearrange("s t (m r) -> s t m r", r=4),
                                      in_=src[0:STEPS, :].rearrange("s (m t r) -> s t m r", t=4, r=4))
                if MODE == "D":
                    nc.vector.tensor_copy(out=rows32[BDOWN_ROW : BDOWN_ROW + 32, 0, :], in_=src[BDOWN_ROW : BDOWN_ROW + 32, 0:P])
                c_bank = psum.tile([P, 4, P], F32, name="t_bank", bufs=BUFS["t_bank"])
                for tt in range(4):
                    nc.tensor.transpose(c_bank[:, tt, :], rows32[:, tt, :], ident[:])
                nc.vector.tensor_copy(out=consts[:], in_=c_bank[:, :, 0 : BDOWN_ROW + 32])
                t["consts"] = consts

        def perm(s):
            e, g = divmod(s, GROUPS)
            words = work.tile([P, 8 * 256], U8, name="upw", bufs=2, align_bytes=64)
            nc.vector.tensor_copy(
                out=words[:].bitcast(I32).rearrange("p (t km w) -> p t km w", t=4, w=2),
                in_=t["upw_raw", s][:].rearrange("p k n -> p (k n)").bitcast(I32).rearrange("p (km t w) -> p t km w", t=4, w=2),
            )
            scales = work.tile([P, 8 * P], U8, name="ups", bufs=2, align_bytes=64)
            nc.vector.tensor_copy(
                out=scales[:].bitcast(I32).rearrange("p (t k m) -> p t k m", t=4, k=2),
                in_=t["us", e][:, :, KP * g : KP * (g + 1)].bitcast(I32).rearrange("p k (m t) -> p t k m", t=4),
            )
            t["upw", s] = words
            t["ups", s] = scales

        def mix(copy, dst, src):
            copy(out=dst.rearrange("p (c i) t -> p c t i", i=4), in_=src.rearrange("p t (c i) -> p c t i", i=4))

        def d_v(s):
            mixed = work.tile([P, D, 4], BF16, name="d_mix", bufs=BUFS["d_mix"], align_bytes=64)
            t["d_mix", s] = mixed
            n = V_COLS[s]
            mix(nc.vector.tensor_copy, mixed[:, 0:n, :], t["d_raw", s][:, :, 0:n])

        def d_s(s, part):
            n = V_COLS[s]
            mid = (n + D) // 16 * 8
            cols = slice(n, mid) if part == 0 else slice(mid, D)
            if n < D:
                mix(nc.scalar.copy, t["d_mix", s][:, cols, :], t["d_raw", s][:, :, cols])

        def d_q(s, h):
            if h == 0:
                t["dc", s] = work.tile([P, D], U32, name="dc", bufs=BUFS["dc"], align_bytes=64)
                t["ds", s] = work.tile([P, D], U8, name="ds", bufs=BUFS["dc"], align_bytes=64)
            cols = slice(KP * h, KP * (h + 1))
            nc.vector.quantize_mx(out=t["dc", s][:, cols].bitcast(FP8X4), scales=t["ds", s][:, cols],
                                  in_=t["d_mix", s][:, cols, :].rearrange("p d t -> p (d t)"))

        def m1(s, half):
            e = s // GROUPS
            xs = t["xs", e]
            x0 = 0 if e == 0 else C * (e - 1)
            for tt in (2 * half, 2 * half + 1):
                bank = psum.tile([P, C], F32, name="h_bank", bufs=BUFS["h_bank"])
                t["h_bank", s, tt] = bank
                for j in range(TILES):
                    for k in range(2):
                        slot = 2 * tt + k
                        nc.tensor.matmul_mx(
                            out=bank[:, P * j : P * (j + 1)],
                            lhsT=t["upw", s][:, 256 * slot : 256 * (slot + 1)].bitcast(FP4X4),
                            lhsT_scale=t["ups", s][:, P * slot : P * (slot + 1)],
                            rhs=t["xw", e][:, k, P * j : P * (j + 1)].bitcast(FP8X4),
                            rhs_scale=xs[:, k, x0 + P * j : x0 + P * (j + 1)],
                            start=(k == 0), stop=(k == 1))

        def h_out(s, half):
            if half == 0:
                t["h_sb", s] = work.tile([P, 4, C], BF16, name="h_sb", bufs=2)
            h = t["h_sb", s]
            for tt in (2 * half, 2 * half + 1):
                nc.scalar.activation(out=h[:, tt, :], in_=t["h_bank", s, tt][:], func=ACT.Relu,
                                     bias=t["consts"][:, tt, s : s + 1])

        def h_mix(s):
            mixed = work.tile([P, C, 4], BF16, name="h_mixed", bufs=2, align_bytes=64)
            t["h_mix", s] = mixed
            mix(nc.vector.tensor_copy, mixed[:], t["h_sb", s][:])

        def h_q(s):
            codes = work.tile([P, C], U32, name="hc", bufs=BUFS["hc"], align_bytes=64)
            scales = work.tile([P, C], U8, name="hs", bufs=BUFS["hc"], align_bytes=64)
            t["hc", s] = codes
            t["hs", s] = scales
            for cols in (slice(0, 256), slice(256, C)):
                nc.vector.quantize_mx(out=codes[:, cols].bitcast(FP8X4), scales=scales[:, cols],
                                      in_=t["h_mix", s][:, cols, :].rearrange("p c t -> p (c t)"))

        def s2(o):
            e, j = divmod(o, TILES)
            base = work.tile([P, D], F32, name="base", bufs=BUFS["base"])
            t["base", o] = base
            nc.vector.scalar_tensor_tensor(out=base[:], in0=t["b_bc", e][:], scalar=t["consts"][:, 0, GATE_ROW + o : GATE_ROW + o + 1],
                                           in1=t["skip", e][:, j, :], op0=ALU.mult, op1=ALU.add)

        def m2(o, h):
            e, j = divmod(o, TILES)
            bank = psum.tile([P, KP], F32, name="o_bank", bufs=BUFS["o_bank"])
            t["o_bank", o, h] = bank
            for g in range(GROUPS):
                s = GROUPS * e + g
                nc.tensor.matmul_mx(
                    out=bank[:],
                    lhsT=t["hc", s][:, P * j : P * (j + 1)].bitcast(FP8X4),
                    lhsT_scale=t["hs", s][:, P * j : P * (j + 1)],
                    rhs=t["dc", s][:, KP * h : KP * (h + 1)].bitcast(FP8X4),
                    rhs_scale=t["ds", s][:, KP * h : KP * (h + 1)],
                    start=(g == 0), stop=(g == GROUPS - 1))

        def m2_d(s, n):
            e, part = divmod(s, GROUPS)
            for i in D_TILES[part][n : n + 1]:
                bank = psum.tile([P, C], F32, name="o_bank", bufs=BUFS["o_bank"])
                t["o_bank", e, i] = bank
                for cols in (slice(0, 256), slice(256, C)):
                    for g in range(GROUPS):
                        q = GROUPS * e + g
                        nc.tensor.matmul_mx(
                            out=bank[:, cols],
                            lhsT=t["dc", q][:, P * i : P * (i + 1)].bitcast(FP8X4),
                            lhsT_scale=t["ds", q][:, P * i : P * (i + 1)],
                            rhs=t["hc", q][:, cols].bitcast(FP8X4),
                            rhs_scale=t["hs", q][:, cols],
                            start=(g == 0), stop=(g == GROUPS - 1))

        def o_out(s, n):
            e, part = divmod(s, GROUPS)
            if part == 0 and n == 0:
                t["ot", e] = work.tile([P, D // P, C], F32, name="ot", bufs=BUFS["ot"])
            for i in D_TILES[part][n : n + 1]:
                row = BDOWN_ROW + 8 * e + i
                nc.scalar.activation(out=t["ot", e][:, i, :], in_=t["o_bank", e, i][:], func=ACT.Identity,
                                     bias=t["consts"][:, 0, row : row + 1])

        def back(o, h):
            e, j = divmod(o, TILES)
            bank = psum.tile([P, KP], F32, name="b_bank", bufs=BUFS["b_bank"])
            t["b_bank", o, h] = bank
            for i in range(4):
                nc.tensor.transpose(bank[:, P * i : P * (i + 1)], t["ot", e][:, 4 * h + i, P * j : P * (j + 1)], ident[:])

        def y_out(o, h):
            e, j = divmod(o, TILES)
            if h == 0:
                t["y", o] = work.tile([P, D], F32, name="y_sb", bufs=BUFS["y_sb"])
            cols = slice(KP * h, KP * (h + 1))
            nc.vector.scalar_tensor_tensor(out=t["y", o][:, cols], in0=t["b_bank" if MODE == "D" else "o_bank", o, h][:],
                                           scalar=t["consts"][:, 0, GATE_ROW + o : GATE_ROW + o + 1],
                                           in1=t["skip", e][:, j, cols] if MODE == "D" else t["base", o][:, cols], op0=ALU.mult, op1=ALU.add)

        def cast(o):
            t["y16", o] = work.tile([P, D], BF16, name="y16", bufs=2)
            copy = nc.vector.tensor_copy if o in CAST_V else nc.scalar.copy
            copy(out=t["y16", o][:], in_=t["y", o][:])

        def turn(o):
            bank = psum.tile([P, 4, P], F32, name="t_bank", bufs=BUFS["t_bank"])
            t["t_bank", o] = bank
            words = t["y16", o][:].bitcast(F32)
            for g in range(2):
                for u in range(2):
                    nc.tensor.transpose(bank[:, 2 * g + u, :], words[:, 256 * g + u : 256 * (g + 1) : 2], ident[:])

        def turn_out(o):
            mixed = work.tile([P, 2, P * 4], BF16, name="y_mix", bufs=2, align_bytes=64)
            t["y_mix", o] = mixed
            nc.scalar.copy(out=mixed[:].bitcast(F32).rearrange("p g (c u) -> p g c u", u=2),
                           in_=t["t_bank", o][:].rearrange("p (g u) c -> p g c u", u=2))

        def y_q(o):
            e, j = divmod(o, TILES)
            if j == 0:
                t["yc", e] = work.tile([P, 2, C], U32, name="yc", bufs=2, align_bytes=64)
            ys = ys_last if e == E - 1 else ys_head
            y0 = P * j if e == E - 1 else P * o
            for g in range(2):
                nc.vector.quantize_mx(out=t["yc", e][:, g, P * j : P * (j + 1)].bitcast(FP8X4),
                                      scales=ys[:, g, y0 : y0 + P], in_=t["y_mix", o][:, g, :])

        def store_y(o):
            e, j = divmod(o, TILES)
            nc.sync.dma_start(out=out_0[e, P * j : P * (j + 1), :], in_=t["y", o][:])

        def store_planes(o):
            e, j = divmod(o, TILES)
            if j == TILES - 1:
                nc.sync.dma_start(out=yw_hbm[:, :, 4 * C * e : 4 * C * (e + 1)].bitcast(I32), in_=t["yc", e][:].bitcast(I32))
                if e == E - 2:
                    move_scale_rows(nc.sync, ys_head, out_2, slice(0, C * (E - 1)), True)
                if e == E - 1:
                    move_scale_rows(nc.sync, ys_last, out_2, slice(C * (E - 1), C * E), True)

        tasks = {
            "load_down": load_down, "load_up": load_up, "load_x": load_x, "load_us": load_us, "load_xs": load_xs, "load_consts": load_consts, "consts": make_consts,

            "m20": lambda s: m2_d(s, 0), "m21": lambda s: m2_d(s, 1), "m22": lambda s: m2_d(s, 2),
            "oo0": lambda s: o_out(s, 0), "oo1": lambda s: o_out(s, 1), "oo2": lambda s: o_out(s, 2),
            "back0": lambda s: back(s, 0), "back1": lambda s: back(s, 1),
            "d_s0": lambda s: d_s(s, 0), "d_s1": lambda s: d_s(s, 1), "m1a": lambda s: m1(s, 0), "m1b": lambda s: m1(s, 1),
            "h_out0": lambda s: h_out(s, 0), "h_out1": lambda s: h_out(s, 1),
            "load_skip": load_skip,
            "perm": perm, "d_v": d_v, "dq0": lambda s: d_q(s, 0), "dq1": lambda s: d_q(s, 1),
            "h_mix": h_mix, "h_q": h_q, "s2": s2,
            "m2a": lambda o: m2(o, 0), "m2b": lambda o: m2(o, 1), "y0": lambda o: y_out(o, 0), "y1": lambda o: y_out(o, 1),
            "cast": cast, "turn": turn, "turn_out": turn_out, "y_q": y_q, "store_y": store_y, "store_planes": store_planes,
        }

        nc.vector.memset(us_raw[0][:].bitcast(I32), 0)
        nc.vector.memset(xs_first[:].bitcast(I32), 0)
        nc.vector.memset(rows32[:], 0.0)
        nc.vector.memset(us_raw[1][:].bitcast(I32), 0)
        nc.vector.memset(xs_rest[:].bitcast(I32), 0)
        make_identity(nc, ident[:])

        for step in range(-6, STEPS + 9):
            for name, lag in ORDER:
                i = step - lag
                if 0 <= i < STEPS:
                    tasks[name](i)
